import numpy as np
import ml_dtypes


def mxq(x, axis, fmt="e4m3"):
    dtype, down = {"e4m3": (ml_dtypes.float8_e4m3fn, 7), "e5m2": (ml_dtypes.float8_e5m2, 14)}[fmt]
    v = np.moveaxis(np.asarray(x, np.float32).astype(ml_dtypes.bfloat16).astype(np.float64), axis, -1)
    blocks = v.reshape(v.shape[:-1] + (-1, 32))
    amax = np.abs(blocks).max(-1, keepdims=True)
    byte = np.maximum(np.where(amax > 0, np.frexp(amax)[1] - 1 + 127, 0) - down, 1)
    scale = np.exp2(byte - 127.0)
    codes = (blocks / scale).astype(np.float32).astype(dtype).astype(np.float64)
    return np.moveaxis((codes * scale).reshape(v.shape), -1, axis)


WIDE = False


def mx_kscale(k):
    if not WIDE:
        return np.ones(k)
    levels = np.array([10, -10, 5, -5, 0])
    if k % 512:
        return np.exp2(np.random.permutation(np.resize(levels, k // 32))).repeat(32)
    a = np.empty((k // 512, 16))
    for p in range(k // 512):
        a[p, :8] = np.random.permutation(np.resize(levels, 8))
        for g in range(8):
            far = levels[np.abs(levels - a[p, g]) >= 10]
            a[p, g + 8] = far[np.random.randint(len(far))]
    return np.exp2(a.ravel()).repeat(32)


def f64(x):
    return np.asarray(x).astype(np.float64)


def striped(idx):
    return np.tile(np.asarray(idx).reshape(-1, 16).T, (8, 1)).astype(np.uint16)


def unstriped(offs):
    return offs[:16].T.reshape(-1).astype(np.int64)


E2M1 = np.array([0.0, 0.5, 1.0, 1.5, 2.0, 3.0, 4.0, 6.0, -0.0, -0.5, -1.0, -1.5, -2.0, -3.0, -4.0, -6.0])


def pack_weight(w, fmt):
    k, n = w.shape
    w = f64(np.asarray(w, np.float32).astype(ml_dtypes.bfloat16)).reshape(k // 32, 32, n)
    amax = np.abs(w).max(1)
    if fmt == "e4m3":
        byte = np.frexp(amax)[1] - 1 + 127 - 7
    else:
        mant, ex = np.frexp(amax / 6.0)
        byte = np.where(mant > 0.5, ex, ex - 1) + 127
    byte = np.clip(np.where(amax > 0, byte, 1), 1, 254)
    scaled = (w * np.exp2(127.0 - byte)[:, None, :]).reshape(k, n).astype(np.float32)
    by_word = np.ascontiguousarray(scaled.reshape(k // 512, 128, 4, n).transpose(0, 1, 3, 2))
    if fmt == "e4m3":
        words = by_word.astype(ml_dtypes.float8_e4m3fn).view(np.uint8)
    else:
        c = by_word.astype(ml_dtypes.float4_e2m1fn).view(np.uint8) & 0xF
        words = (c[..., 0::2] | (c[..., 1::2] << 4)).reshape(k // 512, 128, 2 * n)
    return np.ascontiguousarray(words), np.ascontiguousarray(byte.astype(np.uint8).reshape(k // 512, 16, n))


def unpack_weight(words, scales, fmt):
    g, _, n = scales.shape
    words = np.ascontiguousarray(words).reshape(g, 128, n, -1)
    if fmt == "e4m3":
        vals = words.view(ml_dtypes.float8_e4m3fn).astype(np.float64)
    else:
        nib = np.empty((g, 128, n, 4), np.uint8)
        nib[..., 0::2] = words & 0xF
        nib[..., 1::2] = words >> 4
        vals = E2M1[nib]
    vals = vals * np.repeat(np.exp2(scales.astype(np.float64) - 127.0), 8, axis=1)[..., None]
    return vals.transpose(0, 1, 3, 2).reshape(g * 512, n)


def sigmoid(v):
    return 1.0 / (1.0 + np.exp(-v))


def bf(x):
    return np.asarray(x, np.float32).astype(ml_dtypes.bfloat16)


def planes(Y):
    r, m = Y.shape
    b = f64(bf(Y)).reshape(r // 32, 32, m)
    amax = np.abs(b).max(1)
    byte = np.clip(np.where(amax > 0, np.frexp(amax)[1] - 1 + 127 - 7, 1), 1, 254)
    codes = (b * np.exp2(127.0 - byte)[:, None, :]).reshape(r, m).astype(np.float32).astype(ml_dtypes.float8_e4m3fn).view(np.uint8)
    words = codes.reshape(r // 512, 128, 4, m).transpose(0, 1, 3, 2)
    return np.ascontiguousarray(words), np.ascontiguousarray(byte.astype(np.uint8).reshape(r // 512, 16, m))


K, U, I, T, E = 512, 2048, 512, 1024, 512


def setup_inputs():
    n = np.random.standard_normal
    idx = np.random.permutation(T)[:I]
    idx2 = np.random.permutation(U)[:I]
    fk = mx_kscale(K)
    hidp = pack_weight(n((K, U)) / fk[:, None], "e4m3")
    return {
        "wv": (n((K, E)) * 1 / np.sqrt(K) * fk[:, None]).astype(np.float32),
        "hid_words": hidp[0],
        "hid_scales": hidp[1],
        "store": (n((E, T))).astype(np.float32),
        "rate": (np.random.uniform(0.3, 1.0, (1, I))).astype(np.float32),
        "offs": striped(idx),
        "offs2": striped(idx2),
    }


def reference(wv, hid_words, hid_scales, store, rate, offs, offs2):
    idx = unstriped(offs)
    idx2 = unstriped(offs2)
    hidu = unpack_weight(hid_words, hid_scales, "e4m3")
    wvq = mxq(f64(wv), 0, "e4m3")
    hididx2g = hidu[:, idx2]
    v = wvq.T @ hididx2g
    dl = (v - f64(store)[:, idx]) * f64(rate) * sigmoid(f64(store)[:, idx])
    df = np.zeros((E, T))
    df[:, idx] = dl
    y = f64(store) + df
    words, scales = planes(y)
    return y, words, scales

@@ -1,0 +1,195 @@
+from contextlib import ExitStack
+
+import concourse.mybir as mybir
+from concourse.masks import make_identity
+
+K, U, I, T, E = 512, 2048, 512, 1024, 512
+FLOPS = 2 * K * E * I
+
+F32 = mybir.dt.float32
+BF16 = mybir.dt.bfloat16
+I32 = mybir.dt.int32
+U32 = mybir.dt.uint32
+U16 = mybir.dt.uint16
+U8 = mybir.dt.uint8
+FP8X4 = mybir.dt.float8_e4m3fn_x4
+ALU = mybir.AluOpType
+ACT = mybir.ActivationFunctionType
+
+P = 128
+PACK = 4
+HALF_I = I // 2
+HALF_T = T // 2
+
+
+def tile_attend_storeblend_pl_kernel(tc, wv, hid_words, hid_scales, store, rate, offs, offs2, out_0, out_1, out_2):
+    nc = tc.nc
+    with ExitStack() as ctx:
+        keep = ctx.enter_context(tc.tile_pool(name="keep", bufs=1))
+        psum = ctx.enter_context(tc.psum_pool(name="psum", bufs=1))
+
+        places = keep.tile([P, I // 16], U16, name="places")
+        tokens = keep.tile([P, I // 16], U16, name="tokens")
+        w_raw = keep.tile([P, PACK, E], F32, name="w_raw")
+        h_words = keep.tile([P, U], U32, name="h_words", align_bytes=64)
+        h_scales = keep.tile([P, U], U8, name="h_scales", align_bytes=64)
+        rate_cols = keep.tile([P, PACK], F32, name="rate_cols")
+        old = [keep.tile([P, T], F32, name="old%d" % j) for j in range(PACK)]
+        delta = [keep.tile([P, T], F32, name="delta%d" % j) for j in range(PACK)]
+        store_rows = store.rearrange("(p j) t -> j p t", j=PACK)
+        out_rows = out_0.rearrange("(p j) t -> j p t", j=PACK)
+
+        nc.gpsimd.memset(h_scales[:].bitcast(I32), 0)
+        nc.sync.dma_start(places[:], offs)
+        nc.sync.dma_start(old[0][:], store_rows[0])
+        nc.sync.dma_start(tokens[:], offs2)
+        nc.sync.dma_start(w_raw[:], wv.rearrange("(p j) e -> p j e", j=PACK))
+        for q in range(4):
+            nc.scalar.dma_start(
+                h_scales[32 * q : 32 * q + 4, :].bitcast(I32), hid_scales[0, 4 * q : 4 * q + 4, :].bitcast(I32)
+            )
+        nc.gpsimd.dma_start(rate_cols[:], rate.rearrange("o (p c) -> p (o c)", c=PACK))
+        nc.sync.dma_start(old[1][:], store_rows[1])
+        nc.sync.dma_start(old[2][:], store_rows[2])
+        nc.sync.dma_start(h_words[:].bitcast(I32), hid_words[0].rearrange("p u r -> p (u r)").bitcast(I32))
+        nc.sync.dma_start(old[3][:], store_rows[3])
+        for j in range(PACK):
+            nc.vector.memset(delta[j][:], 0.0)
+
+        identity = keep.tile([P, P], F32, name="identity")
+        make_identity(nc, identity[:])
+        rate_bank = psum.tile([P, PACK, P], F32, name="rate_bank")
+        for c in range(PACK):
+            nc.tensor.transpose(rate_bank[:, c, :], rate_cols[:, c : c + 1].to_broadcast([P, P]), identity[:])
+        rate_row = keep.tile([P, I], F32, name="rate_row")
+        nc.vector.tensor_copy(
+            rate_row[:].rearrange("p (n c) -> p n c", c=PACK), rate_bank[:].rearrange("p c n -> p n c")
+        )
+
+        w_grouped = keep.tile([P, PACK * E], BF16, name="w_grouped", align_bytes=64)
+        w_codes = keep.tile([P, E], U32, name="w_codes", align_bytes=64)
+        w_scales = keep.tile([P, E], U8, name="w_scales", align_bytes=64)
+        g_words = keep.tile([P, I], U32, name="g_words", align_bytes=64)
+        g_scales = keep.tile([P, I], U8, name="g_scales", align_bytes=64)
+        nc.vector.tensor_copy(g_scales[:], h_scales[:].indirect(tokens[:]))
+        nc.vector.tensor_copy(
+            w_grouped[:].rearrange("p (t m j) -> p m j t", t=PACK, j=PACK),
+            w_raw[:].rearrange("p j (m t) -> p m j t", t=PACK),
+        )
+        nc.vector.quantize_mx(out=w_codes[:].bitcast(FP8X4), scales=w_scales[:], in_=w_grouped[:])
+
+        picked = [keep.tile([P, I], F32, name="picked%d" % j) for j in range(PACK)]
+        gate = [keep.tile([P, I], F32, name="gate%d" % j) for j in range(PACK)]
+        weight = [keep.tile([P, I], F32, name="weight%d" % j) for j in range(PACK)]
+        diff = [keep.tile([P, I], F32, name="diff%d" % j) for j in range(PACK)]
+        step = [keep.tile([P, I], F32, name="step%d" % j) for j in range(PACK)]
+        first = [psum.tile([P, HALF_I], F32, name="first%d" % h) for h in range(2)]
+        values = [None] + [psum.tile([P, I], F32, name="values%d" % j) for j in range(1, PACK)]
+        new = keep.tile([P, 2, PACK, HALF_T], F32, name="new")
+
+        def pick(j):
+            nc.scalar.activation(picked[j][:], old[j][:].indirect(places[:]), ACT.Copy)
+            nc.scalar.activation(gate[j][:], picked[j][:], ACT.Sigmoid)
+
+        def weigh(j):
+            nc.vector.tensor_tensor(weight[j][:], gate[j][:], rate_row[:], ALU.mult)
+
+        def weigh_late(j):
+            nc.vector.tensor_tensor(weight[j][:], diff[j][:], rate_row[:], ALU.mult)
+            nc.vector.tensor_tensor(step[j][:], weight[j][:], gate[j][:], ALU.mult)
+
+        def project(bank, j, slots):
+            nc.tensor.matmul_mx(
+                out=bank,
+                lhsT=w_codes[:, j * P : (j + 1) * P].bitcast(FP8X4),
+                lhsT_scale=w_scales[:, j * P : (j + 1) * P],
+                rhs=g_words[:, slots].bitcast(FP8X4),
+                rhs_scale=g_scales[:, slots],
+                start=True,
+                stop=True,
+            )
+
+        def differ(j):
+            nc.vector.tensor_tensor(diff[j][:], values[j][:], picked[j][:], ALU.subtract)
+
+        def cols(h):
+            return slice(h * HALF_I, (h + 1) * HALF_I)
+
+        def listed(h):
+            return places[:, h * HALF_I // 16 : (h + 1) * HALF_I // 16]
+
+        def scatter_vector(j):
+            nc.vector.tensor_tensor(delta[j][:].indirect(places[:]), diff[j][:], weight[j][:], ALU.mult)
+
+        def product(j):
+            nc.vector.tensor_tensor(step[j][:], diff[j][:], weight[j][:], ALU.mult)
+
+        def scatter_scalar(j):
+            for h in range(2):
+                nc.scalar.activation(delta[j][:].indirect(listed(h)), step[j][:, cols(h)], ACT.Copy)
+
+        def blend(j):
+            nc.vector.tensor_tensor(
+                new[:, :, j, :],
+                old[j][:].rearrange("p (h t) -> p h t", h=2),
+                delta[j][:].rearrange("p (h t) -> p h t", h=2),
+                ALU.add,
+            )
+            nc.sync.dma_start(out_rows[j].rearrange("p (h t) -> p h t", h=2), new[:, :, j, :])
+
+        def blend_half(j, h):
+            part = slice(h * HALF_T, (h + 1) * HALF_T)
+            nc.vector.tensor_tensor(new[:, h, j, :], old[j][:, part], delta[j][:, part], ALU.add)
+            nc.sync.dma_start(out_rows[j][:, part], new[:, h, j, :])
+
+        pick(0)
+        weigh(0)
+        pick(1)
+        weigh(1)
+        pick(2)
+        pick(3)
+        for h in range(2):
+            slots = tokens[:, h * HALF_I // 16 : (h + 1) * HALF_I // 16]
+            nc.vector.tensor_copy(g_words[:, cols(h)], h_words[:].indirect(slots))
+            project(first[h][:], 0, cols(h))
+        for j in (2, 1, 3):
+            project(values[j][:], j, slice(0, I))
+        for h in range(2):
+            nc.vector.tensor_tensor(diff[0][:, cols(h)], first[h][:], picked[0][:, cols(h)], ALU.subtract)
+        product(0)
+        scatter_scalar(0)
+        differ(2)
+        weigh_late(2)
+        scatter_scalar(2)
+        differ(1)
+        scatter_vector(1)
+        differ(3)
+        weigh_late(3)
+        scatter_scalar(3)
+        blend(0)
+        blend(1)
+        blend(2)
+        blend_half(3, 0)
+        blend_half(3, 1)
+
+        y_codes = keep.tile([P, T], U32, name="y_codes", align_bytes=64)
+        y_scales = keep.tile([P, T], U8, name="y_scales", align_bytes=64)
+        words_out = out_1[0].rearrange("p t r -> p (t r)").bitcast(I32)
+        split = [384, 192]
+        for h in range(2):
+            grouped = keep.tile([P, PACK * HALF_T], BF16, name="grouped%d" % h, align_bytes=64)
+            n = split[h]
+            nc.scalar.copy(
+                grouped[:, : PACK * n].rearrange("p (c i j) -> p c j i", i=4, j=PACK),
+                new[:, h, :, :n].rearrange("p j (c i) -> p c j i", i=4),
+            )
+            nc.vector.tensor_copy(
+                grouped[:, PACK * n :].rearrange("p (c i j) -> p c j i", i=4, j=PACK),
+                new[:, h, :, n:].rearrange("p j (c i) -> p c j i", i=4),
+            )
+            part = slice(h * HALF_T, (h + 1) * HALF_T)
+            nc.vector.quantize_mx(out=y_codes[:, part].bitcast(FP8X4), scales=y_scales[:, part], in_=grouped[:])
+            nc.sync.dma_start(words_out[:, part], y_codes[:, part].bitcast(I32))
+        for q in range(4):
+            queue = nc.scalar if q % 2 else nc.sync
+            queue.dma_start(out_2[0, 4 * q : 4 * q + 4, :].bitcast(I32), y_scales[32 * q : 32 * q + 4, :].bitcast(I32))

@@ -48,7 +48,7 @@ def tile_attend_storeblend_pl_kernel(tc, wv, hid_words, hid_scales, store, rate,
             nc.scalar.dma_start(
                 h_scales[32 * q : 32 * q + 4, :].bitcast(I32), hid_scales[0, 4 * q : 4 * q + 4, :].bitcast(I32)
             )
-        nc.gpsimd.dma_start(rate_cols[:], rate.rearrange("o (p c) -> p (o c)", c=PACK))
+        nc.sync.dma_start(rate_cols[:], rate.rearrange("o (p c) -> p (o c)", c=PACK))
         nc.sync.dma_start(old[1][:], store_rows[1])
         nc.sync.dma_start(old[2][:], store_rows[2])
         nc.sync.dma_start(h_words[:].bitcast(I32), hid_words[0].rearrange("p u r -> p (u r)").bitcast(I32))
@@ -94,9 +94,8 @@ def tile_attend_storeblend_pl_kernel(tc, wv, hid_words, hid_scales, store, rate,
         def weigh(j):
             nc.vector.tensor_tensor(weight[j][:], gate[j][:], rate_row[:], ALU.mult)
 
-        def weigh_late(j):
+        def rated(j):
             nc.vector.tensor_tensor(weight[j][:], diff[j][:], rate_row[:], ALU.mult)
-            nc.vector.tensor_tensor(step[j][:], weight[j][:], gate[j][:], ALU.mult)
 
         def project(bank, j, slots):
             nc.tensor.matmul_mx(
@@ -115,18 +114,17 @@ def tile_attend_storeblend_pl_kernel(tc, wv, hid_words, hid_scales, store, rate,
         def cols(h):
             return slice(h * HALF_I, (h + 1) * HALF_I)
 
-        def listed(h):
-            return places[:, h * HALF_I // 16 : (h + 1) * HALF_I // 16]
+        def listed(a, b):
+            return places[:, a // 16 : b // 16]
 
-        def scatter_vector(j):
-            nc.vector.tensor_tensor(delta[j][:].indirect(places[:]), diff[j][:], weight[j][:], ALU.mult)
+        def scatter_vector(j, other, a, b):
+            nc.vector.tensor_tensor(delta[j][:].indirect(listed(a, b)), other[:, a:b], weight[j][:, a:b], ALU.mult)
 
-        def product(j):
-            nc.vector.tensor_tensor(step[j][:], diff[j][:], weight[j][:], ALU.mult)
+        def product(j, other, a, b):
+            nc.vector.tensor_tensor(step[j][:, a:b], other[:, a:b], weight[j][:, a:b], ALU.mult)
 
-        def scatter_scalar(j):
-            for h in range(2):
-                nc.scalar.activation(delta[j][:].indirect(listed(h)), step[j][:, cols(h)], ACT.Copy)
+        def scatter_scalar(j, a, b):
+            nc.scalar.activation(delta[j][:].indirect(listed(a, b)), step[j][:, a:b], ACT.Copy)
 
         def blend(j):
             nc.vector.tensor_tensor(
@@ -152,20 +150,26 @@ def tile_attend_storeblend_pl_kernel(tc, wv, hid_words, hid_scales, store, rate,
             slots = tokens[:, h * HALF_I // 16 : (h + 1) * HALF_I // 16]
             nc.vector.tensor_copy(g_words[:, cols(h)], h_words[:].indirect(slots))
             project(first[h][:], 0, cols(h))
-        for j in (2, 1, 3):
+        for j in (2, 3, 1):
             project(values[j][:], j, slice(0, I))
         for h in range(2):
             nc.vector.tensor_tensor(diff[0][:, cols(h)], first[h][:], picked[0][:, cols(h)], ALU.subtract)
-        product(0)
-        scatter_scalar(0)
+        product(0, diff[0], 0, HALF_I)
+        product(0, diff[0], HALF_I, I)
+        scatter_scalar(0, 0, HALF_I)
+        scatter_scalar(0, HALF_I, I)
         differ(2)
-        weigh_late(2)
-        scatter_scalar(2)
-        differ(1)
-        scatter_vector(1)
         differ(3)
-        weigh_late(3)
-        scatter_scalar(3)
+        rated(2)
+        rated(3)
+        product(2, gate[2], 0, I)
+        scatter_scalar(2, 0, HALF_I)
+        scatter_scalar(2, HALF_I, I)
+        differ(1)
+        product(3, gate[3], 0, I)
+        scatter_scalar(3, 0, HALF_I)
+        scatter_scalar(3, HALF_I, I)
+        scatter_vector(1, diff[1], 0, I)
         blend(0)
         blend(1)
         blend(2)
@@ -175,21 +179,27 @@ def tile_attend_storeblend_pl_kernel(tc, wv, hid_words, hid_scales, store, rate,
         y_codes = keep.tile([P, T], U32, name="y_codes", align_bytes=64)
         y_scales = keep.tile([P, T], U8, name="y_scales", align_bytes=64)
         words_out = out_1[0].rearrange("p t r -> p (t r)").bitcast(I32)
-        split = [384, 192]
-        for h in range(2):
-            grouped = keep.tile([P, PACK * HALF_T], BF16, name="grouped%d" % h, align_bytes=64)
-            n = split[h]
-            nc.scalar.copy(
-                grouped[:, : PACK * n].rearrange("p (c i j) -> p c j i", i=4, j=PACK),
-                new[:, h, :, :n].rearrange("p j (c i) -> p c j i", i=4),
+        grouped = keep.tile([P, PACK * T], BF16, name="grouped", align_bytes=64)
+
+        def interleave(copy, a, b):
+            h, lo = divmod(a, HALF_T)
+            copy(
+                grouped[:, PACK * a : PACK * b].rearrange("p (c i j) -> p c j i", i=4, j=PACK),
+                new[:, h, :, lo : lo + b - a].rearrange("p j (c i) -> p c j i", i=4),
             )
-            nc.vector.tensor_copy(
-                grouped[:, PACK * n :].rearrange("p (c i j) -> p c j i", i=4, j=PACK),
-                new[:, h, :, n:].rearrange("p j (c i) -> p c j i", i=4),
+
+        def quantize(a, b):
+            nc.vector.quantize_mx(
+                out=y_codes[:, a:b].bitcast(FP8X4), scales=y_scales[:, a:b], in_=grouped[:, PACK * a : PACK * b]
             )
-            part = slice(h * HALF_T, (h + 1) * HALF_T)
-            nc.vector.quantize_mx(out=y_codes[:, part].bitcast(FP8X4), scales=y_scales[:, part], in_=grouped[:])
-            nc.sync.dma_start(words_out[:, part], y_codes[:, part].bitcast(I32))
+
+        interleave(nc.scalar.copy, 0, 384)
+        interleave(nc.vector.tensor_copy, 384, 512)
+        interleave(nc.vector.tensor_copy, 512, 768)
+        interleave(nc.scalar.copy, 768, 1024)
+        for a, b in ((0, 512), (512, 768), (768, 1024)):
+            quantize(a, b)
+            nc.sync.dma_start(words_out[:, a:b], y_codes[:, a:b].bitcast(I32))
         for q in range(4):
-            queue = nc.scalar if q % 2 else nc.sync
+            queue = nc.sync if q % 2 else nc.scalar
             queue.dma_start(out_2[0, 4 * q : 4 * q + 4, :].bitcast(I32), y_scales[32 * q : 32 * q + 4, :].bitcast(I32))

@@ -30,8 +30,8 @@ def tile_attend_storeblend_pl_kernel(tc, wv, hid_words, hid_scales, store, rate,
 
         places = keep.tile([P, I // 16], U16, name="places")
         tokens = keep.tile([P, I // 16], U16, name="tokens")
-        w_raw = keep.tile([P, PACK, E], F32, name="w_raw")
-        h_words = keep.tile([P, U], U32, name="h_words", align_bytes=64)
+        w_raw = keep.tile([P, PACK, E], F32, name="w_raw", tag="w_raw")
+        h_words = keep.tile([P, U], U32, name="h_words", tag="h_words", align_bytes=64)
         h_scales = keep.tile([P, U], U8, name="h_scales", align_bytes=64)
         rate_cols = keep.tile([P, PACK], F32, name="rate_cols")
         old = [keep.tile([P, T], F32, name="old%d" % j) for j in range(PACK)]
@@ -43,13 +43,13 @@ def tile_attend_storeblend_pl_kernel(tc, wv, hid_words, hid_scales, store, rate,
         nc.sync.dma_start(places[:], offs)
         nc.sync.dma_start(old[0][:], store_rows[0])
         nc.sync.dma_start(tokens[:], offs2)
-        nc.sync.dma_start(w_raw[:], wv.rearrange("(p j) e -> p j e", j=PACK))
+        nc.sync.dma_start(old[1][:], store_rows[1])
         for q in range(4):
             nc.scalar.dma_start(
                 h_scales[32 * q : 32 * q + 4, :].bitcast(I32), hid_scales[0, 4 * q : 4 * q + 4, :].bitcast(I32)
             )
         nc.sync.dma_start(rate_cols[:], rate.rearrange("o (p c) -> p (o c)", c=PACK))
-        nc.sync.dma_start(old[1][:], store_rows[1])
+        nc.sync.dma_start(w_raw[:], wv.rearrange("(p j) e -> p j e", j=PACK))
         nc.sync.dma_start(old[2][:], store_rows[2])
         nc.sync.dma_start(h_words[:].bitcast(I32), hid_words[0].rearrange("p u r -> p (u r)").bitcast(I32))
         nc.sync.dma_start(old[3][:], store_rows[3])
@@ -80,7 +80,12 @@ def tile_attend_storeblend_pl_kernel(tc, wv, hid_words, hid_scales, store, rate,
 
         picked = [keep.tile([P, I], F32, name="picked%d" % j) for j in range(PACK)]
         gate = [keep.tile([P, I], F32, name="gate%d" % j) for j in range(PACK)]
-        weight = [keep.tile([P, I], F32, name="weight%d" % j) for j in range(PACK)]
+        weight = [
+            keep.tile([P, I], F32, name="weight0"),
+            keep.tile([P, I], F32, name="weight1", tag="w_raw"),
+            keep.tile([P, I], F32, name="weight2", tag="h_words", align_bytes=64),
+            keep.tile([P, I], F32, name="weight3"),
+        ]
         diff = [keep.tile([P, I], F32, name="diff%d" % j) for j in range(PACK)]
         step = [keep.tile([P, I], F32, name="step%d" % j) for j in range(PACK)]
         first = [psum.tile([P, HALF_I], F32, name="first%d" % h) for h in range(2)]
@@ -113,6 +118,9 @@ def tile_attend_storeblend_pl_kernel(tc, wv, hid_words, hid_scales, store, rate,
 
         def cols(h):
             return slice(h * HALF_I, (h + 1) * HALF_I)
+
+        def differ_first(h):
+            nc.vector.tensor_tensor(diff[0][:, cols(h)], first[h][:], picked[0][:, cols(h)], ALU.subtract)
 
         def listed(a, b):
             return places[:, a // 16 : b // 16]
@@ -152,22 +160,24 @@ def tile_attend_storeblend_pl_kernel(tc, wv, hid_words, hid_scales, store, rate,
             project(first[h][:], 0, cols(h))
         for j in (2, 3, 1):
             project(values[j][:], j, slice(0, I))
-        for h in range(2):
-            nc.vector.tensor_tensor(diff[0][:, cols(h)], first[h][:], picked[0][:, cols(h)], ALU.subtract)
+        differ_first(0)
+        weigh(2)
         product(0, diff[0], 0, HALF_I)
-        product(0, diff[0], HALF_I, I)
         scatter_scalar(0, 0, HALF_I)
-        scatter_scalar(0, HALF_I, I)
         differ(2)
-        differ(3)
-        rated(2)
-        rated(3)
-        product(2, gate[2], 0, I)
+        differ_first(1)
+        product(2, diff[2], 0, HALF_I)
         scatter_scalar(2, 0, HALF_I)
-        scatter_scalar(2, HALF_I, I)
+        differ(3)
+        product(0, diff[0], HALF_I, I)
+        scatter_scalar(0, HALF_I, I)
+        rated(3)
         differ(1)
-        product(3, gate[3], 0, I)
+        product(3, gate[3], 0, HALF_I)
         scatter_scalar(3, 0, HALF_I)
+        product(2, diff[2], HALF_I, I)
+        scatter_scalar(2, HALF_I, I)
+        product(3, gate[3], HALF_I, I)
         scatter_scalar(3, HALF_I, I)
         scatter_vector(1, diff[1], 0, I)
         blend(0)
@@ -193,8 +203,8 @@ def tile_attend_storeblend_pl_kernel(tc, wv, hid_words, hid_scales, store, rate,
                 out=y_codes[:, a:b].bitcast(FP8X4), scales=y_scales[:, a:b], in_=grouped[:, PACK * a : PACK * b]
             )
 
-        interleave(nc.scalar.copy, 0, 384)
-        interleave(nc.vector.tensor_copy, 384, 512)
+        interleave(nc.scalar.copy, 0, 320)
+        interleave(nc.vector.tensor_copy, 320, 512)
         interleave(nc.vector.tensor_copy, 512, 768)
         interleave(nc.scalar.copy, 768, 1024)
         for a, b in ((0, 512), (512, 768), (768, 1024)):

@@ -39,6 +39,10 @@ def tile_attend_storeblend_pl_kernel(tc, wv, hid_words, hid_scales, store, rate,
         store_rows = store.rearrange("(p j) t -> j p t", j=PACK)
         out_rows = out_0.rearrange("(p j) t -> j p t", j=PACK)
 
+        warm = keep.tile([P, 1], F32, name="warm")
+        warmed = keep.tile([P, 1], F32, name="warmed")
+        nc.gpsimd.memset(warm[:], 0.0)
+        nc.scalar.activation(warmed[:], warm[:], ACT.Sigmoid)
         nc.gpsimd.memset(h_scales[:].bitcast(I32), 0)
         nc.sync.dma_start(places[:], offs)
         nc.sync.dma_start(old[0][:], store_rows[0])

from contextlib import ExitStack

import concourse.mybir as mybir
from concourse.masks import make_identity

K, U, I, T, E = 512, 2048, 512, 1024, 512
FLOPS = 2 * K * E * I

F32 = mybir.dt.float32
BF16 = mybir.dt.bfloat16
I32 = mybir.dt.int32
U32 = mybir.dt.uint32
U16 = mybir.dt.uint16
U8 = mybir.dt.uint8
FP8X4 = mybir.dt.float8_e4m3fn_x4
ALU = mybir.AluOpType
ACT = mybir.ActivationFunctionType

P = 128
PACK = 4
HALF_I = I // 2
HALF_T = T // 2


def tile_attend_storeblend_pl_kernel(tc, wv, hid_words, hid_scales, store, rate, offs, offs2, out_0, out_1, out_2):
    nc = tc.nc
    with ExitStack() as ctx:
        keep = ctx.enter_context(tc.tile_pool(name="keep", bufs=1))
        psum = ctx.enter_context(tc.psum_pool(name="psum", bufs=1))

        places = keep.tile([P, I // 16], U16, name="places")
        tokens = keep.tile([P, I // 16], U16, name="tokens")
        w_raw = keep.tile([P, PACK, E], F32, name="w_raw", tag="w_raw")
        h_words = keep.tile([P, U], U32, name="h_words", tag="h_words", align_bytes=64)
        h_scales = keep.tile([P, U], U8, name="h_scales", align_bytes=64)
        rate_cols = keep.tile([P, PACK], F32, name="rate_cols")
        old = [keep.tile([P, T], F32, name="old%d" % j) for j in range(PACK)]
        delta = [keep.tile([P, T], F32, name="delta%d" % j) for j in range(PACK)]
        store_rows = store.rearrange("(p j) t -> j p t", j=PACK)
        out_rows = out_0.rearrange("(p j) t -> j p t", j=PACK)

        warm = keep.tile([P, 1], F32, name="warm")
        warmed = keep.tile([P, 1], F32, name="warmed")
        nc.gpsimd.memset(warm[:], 0.0)
        nc.scalar.activation(warmed[:], warm[:], ACT.Sigmoid)
        nc.gpsimd.memset(h_scales[:].bitcast(I32), 0)
        nc.sync.dma_start(places[:], offs)
        nc.sync.dma_start(old[0][:], store_rows[0])
        nc.sync.dma_start(tokens[:], offs2)
        nc.sync.dma_start(old[1][:], store_rows[1])
        for q in range(4):
            nc.scalar.dma_start(
                h_scales[32 * q : 32 * q + 4, :].bitcast(I32), hid_scales[0, 4 * q : 4 * q + 4, :].bitcast(I32)
            )
        nc.sync.dma_start(rate_cols[:], rate.rearrange("o (p c) -> p (o c)", c=PACK))
        nc.sync.dma_start(w_raw[:], wv.rearrange("(p j) e -> p j e", j=PACK))
        nc.sync.dma_start(old[2][:], store_rows[2])
        nc.sync.dma_start(h_words[:].bitcast(I32), hid_words[0].rearrange("p u r -> p (u r)").bitcast(I32))
        nc.sync.dma_start(old[3][:], store_rows[3])
        for j in range(PACK):
            nc.vector.memset(delta[j][:], 0.0)

        identity = keep.tile([P, P], F32, name="identity")
        make_identity(nc, identity[:])
        rate_bank = psum.tile([P, PACK, P], F32, name="rate_bank")
        for c in range(PACK):
            nc.tensor.transpose(rate_bank[:, c, :], rate_cols[:, c : c + 1].to_broadcast([P, P]), identity[:])
        rate_row = keep.tile([P, I], F32, name="rate_row")
        nc.vector.tensor_copy(
            rate_row[:].rearrange("p (n c) -> p n c", c=PACK), rate_bank[:].rearrange("p c n -> p n c")
        )

        w_grouped = keep.tile([P, PACK * E], BF16, name="w_grouped", align_bytes=64)
        w_codes = keep.tile([P, E], U32, name="w_codes", align_bytes=64)
        w_scales = keep.tile([P, E], U8, name="w_scales", align_bytes=64)
        g_words = keep.tile([P, I], U32, name="g_words", align_bytes=64)
        g_scales = keep.tile([P, I], U8, name="g_scales", align_bytes=64)
        nc.vector.tensor_copy(g_scales[:], h_scales[:].indirect(tokens[:]))
        nc.vector.tensor_copy(
            w_grouped[:].rearrange("p (t m j) -> p m j t", t=PACK, j=PACK),
            w_raw[:].rearrange("p j (m t) -> p m j t", t=PACK),
        )
        nc.vector.quantize_mx(out=w_codes[:].bitcast(FP8X4), scales=w_scales[:], in_=w_grouped[:])

        picked = [keep.tile([P, I], F32, name="picked%d" % j) for j in range(PACK)]
        gate = [keep.tile([P, I], F32, name="gate%d" % j) for j in range(PACK)]
        weight = [
            keep.tile([P, I], F32, name="weight0"),
            keep.tile([P, I], F32, name="weight1", tag="w_raw"),
            keep.tile([P, I], F32, name="weight2", tag="h_words", align_bytes=64),
            keep.tile([P, I], F32, name="weight3"),
        ]
        diff = [keep.tile([P, I], F32, name="diff%d" % j) for j in range(PACK)]
        step = [keep.tile([P, I], F32, name="step%d" % j) for j in range(PACK)]
        first = [psum.tile([P, HALF_I], F32, name="first%d" % h) for h in range(2)]
        values = [None] + [psum.tile([P, I], F32, name="values%d" % j) for j in range(1, PACK)]
        new = keep.tile([P, 2, PACK, HALF_T], F32, name="new")

        def pick(j):
            nc.scalar.activation(picked[j][:], old[j][:].indirect(places[:]), ACT.Copy)
            nc.scalar.activation(gate[j][:], picked[j][:], ACT.Sigmoid)

        def weigh(j):
            nc.vector.tensor_tensor(weight[j][:], gate[j][:], rate_row[:], ALU.mult)

        def rated(j):
            nc.vector.tensor_tensor(weight[j][:], diff[j][:], rate_row[:], ALU.mult)

        def project(bank, j, slots):
            nc.tensor.matmul_mx(
                out=bank,
                lhsT=w_codes[:, j * P : (j + 1) * P].bitcast(FP8X4),
                lhsT_scale=w_scales[:, j * P : (j + 1) * P],
                rhs=g_words[:, slots].bitcast(FP8X4),
                rhs_scale=g_scales[:, slots],
                start=True,
                stop=True,
            )

        def differ(j):
            nc.vector.tensor_tensor(diff[j][:], values[j][:], picked[j][:], ALU.subtract)

        def cols(h):
            return slice(h * HALF_I, (h + 1) * HALF_I)

        def differ_first(h):
            nc.vector.tensor_tensor(diff[0][:, cols(h)], first[h][:], picked[0][:, cols(h)], ALU.subtract)

        def listed(a, b):
            return places[:, a // 16 : b // 16]

        def scatter_vector(j, other, a, b):
            nc.vector.tensor_tensor(delta[j][:].indirect(listed(a, b)), other[:, a:b], weight[j][:, a:b], ALU.mult)

        def product(j, other, a, b):
            nc.vector.tensor_tensor(step[j][:, a:b], other[:, a:b], weight[j][:, a:b], ALU.mult)

        def scatter_scalar(j, a, b):
            nc.scalar.activation(delta[j][:].indirect(listed(a, b)), step[j][:, a:b], ACT.Copy)

        def blend(j):
            nc.vector.tensor_tensor(
                new[:, :, j, :],
                old[j][:].rearrange("p (h t) -> p h t", h=2),
                delta[j][:].rearrange("p (h t) -> p h t", h=2),
                ALU.add,
            )
            nc.sync.dma_start(out_rows[j].rearrange("p (h t) -> p h t", h=2), new[:, :, j, :])

        def blend_half(j, h):
            part = slice(h * HALF_T, (h + 1) * HALF_T)
            nc.vector.tensor_tensor(new[:, h, j, :], old[j][:, part], delta[j][:, part], ALU.add)
            nc.sync.dma_start(out_rows[j][:, part], new[:, h, j, :])

        pick(0)
        weigh(0)
        pick(1)
        weigh(1)
        pick(2)
        pick(3)
        for h in range(2):
            slots = tokens[:, h * HALF_I // 16 : (h + 1) * HALF_I // 16]
            nc.vector.tensor_copy(g_words[:, cols(h)], h_words[:].indirect(slots))
            project(first[h][:], 0, cols(h))
        for j in (2, 3, 1):
            project(values[j][:], j, slice(0, I))
        differ_first(0)
        weigh(2)
        product(0, diff[0], 0, HALF_I)
        scatter_scalar(0, 0, HALF_I)
        differ(2)
        differ_first(1)
        product(2, diff[2], 0, HALF_I)
        scatter_scalar(2, 0, HALF_I)
        differ(3)
        product(0, diff[0], HALF_I, I)
        scatter_scalar(0, HALF_I, I)
        rated(3)
        differ(1)
        product(3, gate[3], 0, HALF_I)
        scatter_scalar(3, 0, HALF_I)
        product(2, diff[2], HALF_I, I)
        scatter_scalar(2, HALF_I, I)
        product(3, gate[3], HALF_I, I)
        scatter_scalar(3, HALF_I, I)
        scatter_vector(1, diff[1], 0, I)
        blend(0)
        blend(1)
        blend(2)
        blend_half(3, 0)
        blend_half(3, 1)

        y_codes = keep.tile([P, T], U32, name="y_codes", align_bytes=64)
        y_scales = keep.tile([P, T], U8, name="y_scales", align_bytes=64)
        words_out = out_1[0].rearrange("p t r -> p (t r)").bitcast(I32)
        grouped = keep.tile([P, PACK * T], BF16, name="grouped", align_bytes=64)

        def interleave(copy, a, b):
            h, lo = divmod(a, HALF_T)
            copy(
                grouped[:, PACK * a : PACK * b].rearrange("p (c i j) -> p c j i", i=4, j=PACK),
                new[:, h, :, lo : lo + b - a].rearrange("p j (c i) -> p c j i", i=4),
            )

        def quantize(a, b):
            nc.vector.quantize_mx(
                out=y_codes[:, a:b].bitcast(FP8X4), scales=y_scales[:, a:b], in_=grouped[:, PACK * a : PACK * b]
            )

        interleave(nc.scalar.copy, 0, 320)
        interleave(nc.vector.tensor_copy, 320, 512)
        interleave(nc.vector.tensor_copy, 512, 768)
        interleave(nc.scalar.copy, 768, 1024)
        for a, b in ((0, 512), (512, 768), (768, 1024)):
            quantize(a, b)
            nc.sync.dma_start(words_out[:, a:b], y_codes[:, a:b].bitcast(I32))
        for q in range(4):
            queue = nc.sync if q % 2 else nc.scalar
            queue.dma_start(out_2[0, 4 * q : 4 * q + 4, :].bitcast(I32), y_scales[32 * q : 32 * q + 4, :].bitcast(I32))
